import numpy as np
CORES = [0,1,2,3,4,5,6,7]
N = 8
def setup_inputs(rng):
    return {"x": rng.standard_normal((N, 128, 2048), dtype=np.float32)}
def reference(x):
    s = x.min(axis=0)
    return {"y": np.broadcast_to(s, (N,) + s.shape)}

@@ -1,0 +1,53 @@
+from concourse.bass import DstId, RemoteDMATransfer
+
+N = 8
+SCRATCH = {
+    "xs": ("dram", [N, 128, 256], "float32"),
+    "land": ("dram", [N, 128, 256], "float32"),
+    "res": ("dram", [N, 128, 256], "float32"),
+}
+SEMAPHORES = ["loaded", "arrived", "sent", "stored"] + ["done%d" % b for b in range(N)]
+
+
+def rank_program(g, core, T, topo):
+    me = T.rank_of(core)
+    if me is None:
+        return
+    others = [r for r in range(N) if r != me]
+
+    def dst_id(r):
+        rid, pid, _se = topo.addr(T.cores[r])
+        return DstId(rid=rid, pnc=pid)
+
+    g.sync.dma_start(T.xs[:], T.x[:]).then_inc(T.sem.loaded, 16)
+    g.wait_ge(T.sem.loaded, 16)
+
+    g.remote_dma_fused(
+        [RemoteDMATransfer(dst_ids=[dst_id(r)], dma_engine_mask=0x3 << (2 * k), remote_sem=T.sem.arrived,
+                           src=T.xs[r], dst=T.land[me])
+         for k, r in enumerate(others)],
+        local_sem=T.sem.sent)
+    sent = 14
+
+    g.wait_ge(T.sem.arrived, 14)
+    g.remote_dma_fused(
+        [RemoteDMATransfer(dst_ids=[dst_id(r) for r in others], dma_engine_mask=0xFFFF,
+                           remote_sem=T.sem["done%d" % me],
+                           srcs=[T.xs[me]] + [T.land[r] for r in others],
+                           dsts=[T.res[me] for _r in others], alu_op=3)],
+        local_sem=T.sem.sent)
+    sent += 16
+
+    mate = me ^ 1
+    rid, pid, _se = topo.addr(T.cores[mate])
+    g.wait_ge(T.sem["done%d" % mate], 16)
+    g.remote_dma(T.res[mate], T.res[mate], T.sem["done%d" % mate], T.sem.sent, pid, rid,
+                 topo.mask(core, T.cores[mate]))
+    sent += 16
+
+    for b in range(N):
+        g.sync.wait_ge(T.sem["done%d" % b], 16)
+    g.sync.dma_start(T.y[:], T.res[:]).then_inc(T.sem.stored, 16)
+
+    g.wait_ge(T.sem.sent, sent)
+    g.wait_ge(T.sem.stored, 16)

@@ -1,6 +1,7 @@
 from concourse.bass import DstId, RemoteDMATransfer
 
 N = 8
+ROWS = 128 // N
 SCRATCH = {
     "xs": ("dram", [N, 128, 256], "float32"),
     "land": ("dram", [N, 128, 256], "float32"),
@@ -19,6 +20,9 @@ def rank_program(g, core, T, topo):
         rid, pid, _se = topo.addr(T.cores[r])
         return DstId(rid=rid, pnc=pid)
 
+    def done(b):
+        return T.sem["done%d" % b]
+
     g.sync.dma_start(T.xs[:], T.x[:]).then_inc(T.sem.loaded, 16)
     g.wait_ge(T.sem.loaded, 16)
 
@@ -27,12 +31,11 @@ def rank_program(g, core, T, topo):
                            src=T.xs[r], dst=T.land[me])
          for k, r in enumerate(others)],
         local_sem=T.sem.sent)
-    sent = 14
+    sent = 2 * len(others)
 
-    g.wait_ge(T.sem.arrived, 14)
+    g.wait_ge(T.sem.arrived, 2 * len(others))
     g.remote_dma_fused(
-        [RemoteDMATransfer(dst_ids=[dst_id(r) for r in others], dma_engine_mask=0xFFFF,
-                           remote_sem=T.sem["done%d" % me],
+        [RemoteDMATransfer(dst_ids=[dst_id(r) for r in others], dma_engine_mask=0xFFFF, remote_sem=done(me),
                            srcs=[T.xs[me]] + [T.land[r] for r in others],
                            dsts=[T.res[me] for _r in others], alu_op=3)],
         local_sem=T.sem.sent)
@@ -40,14 +43,18 @@ def rank_program(g, core, T, topo):
 
     mate = me ^ 1
     rid, pid, _se = topo.addr(T.cores[mate])
-    g.wait_ge(T.sem["done%d" % mate], 16)
-    g.remote_dma(T.res[mate], T.res[mate], T.sem["done%d" % mate], T.sem.sent, pid, rid,
-                 topo.mask(core, T.cores[mate]))
+    g.wait_ge(done(mate), 16)
+    g.remote_dma(T.res[mate], T.res[mate], done(mate), T.sem.sent, pid, rid, topo.mask(core, T.cores[mate]))
     sent += 16
 
-    for b in range(N):
-        g.sync.wait_ge(T.sem["done%d" % b], 16)
-    g.sync.dma_start(T.y[:], T.res[:]).then_inc(T.sem.stored, 16)
+    stored = 0
+    for q, lo, hi in ((g.sync, 0, me), (g.scalar, me + 1, N), (g.scalar, me, me + 1)):
+        if lo == hi:
+            continue
+        for b in range(lo, hi):
+            q.wait_ge(done(b), 16)
+        q.dma_start(T.y[lo * ROWS:hi * ROWS, :], T.res[lo:hi]).then_inc(T.sem.stored, 16)
+        stored += 16
 
     g.wait_ge(T.sem.sent, sent)
-    g.wait_ge(T.sem.stored, 16)
+    g.wait_ge(T.sem.stored, stored)

from concourse.bass import DstId, RemoteDMATransfer

N = 8
ROWS = 128 // N
SCRATCH = {
    "xs": ("dram", [N, 128, 256], "float32"),
    "land": ("dram", [N, 128, 256], "float32"),
    "res": ("dram", [N, 128, 256], "float32"),
}
SEMAPHORES = ["loaded", "arrived", "sent", "stored"] + ["done%d" % b for b in range(N)]


def rank_program(g, core, T, topo):
    me = T.rank_of(core)
    if me is None:
        return
    others = [r for r in range(N) if r != me]

    def dst_id(r):
        rid, pid, _se = topo.addr(T.cores[r])
        return DstId(rid=rid, pnc=pid)

    def done(b):
        return T.sem["done%d" % b]

    g.sync.dma_start(T.xs[:], T.x[:]).then_inc(T.sem.loaded, 16)
    g.wait_ge(T.sem.loaded, 16)

    g.remote_dma_fused(
        [RemoteDMATransfer(dst_ids=[dst_id(r)], dma_engine_mask=0x3 << (2 * k), remote_sem=T.sem.arrived,
                           src=T.xs[r], dst=T.land[me])
         for k, r in enumerate(others)],
        local_sem=T.sem.sent)
    sent = 2 * len(others)

    g.wait_ge(T.sem.arrived, 2 * len(others))
    g.remote_dma_fused(
        [RemoteDMATransfer(dst_ids=[dst_id(r) for r in others], dma_engine_mask=0xFFFF, remote_sem=done(me),
                           srcs=[T.xs[me]] + [T.land[r] for r in others],
                           dsts=[T.res[me] for _r in others], alu_op=3)],
        local_sem=T.sem.sent)
    sent += 16

    mate = me ^ 1
    rid, pid, _se = topo.addr(T.cores[mate])
    g.wait_ge(done(mate), 16)
    g.remote_dma(T.res[mate], T.res[mate], done(mate), T.sem.sent, pid, rid, topo.mask(core, T.cores[mate]))
    sent += 16

    stored = 0
    for q, lo, hi in ((g.sync, 0, me), (g.scalar, me + 1, N), (g.scalar, me, me + 1)):
        if lo == hi:
            continue
        for b in range(lo, hi):
            q.wait_ge(done(b), 16)
        q.dma_start(T.y[lo * ROWS:hi * ROWS, :], T.res[lo:hi]).then_inc(T.sem.stored, 16)
        stored += 16

    g.wait_ge(T.sem.sent, sent)
    g.wait_ge(T.sem.stored, stored)
